import numpy as np
import ml_dtypes


def mxq(x, axis, fmt="e4m3"):
    dtype, down = {"e4m3": (ml_dtypes.float8_e4m3fn, 7), "e5m2": (ml_dtypes.float8_e5m2, 14)}[fmt]
    v = np.moveaxis(np.asarray(x, np.float32).astype(ml_dtypes.bfloat16).astype(np.float64), axis, -1)
    blocks = v.reshape(v.shape[:-1] + (-1, 32))
    amax = np.abs(blocks).max(-1, keepdims=True)
    byte = np.maximum(np.where(amax > 0, np.frexp(amax)[1] - 1 + 127, 0) - down, 1)
    scale = np.exp2(byte - 127.0)
    codes = (blocks / scale).astype(np.float32).astype(dtype).astype(np.float64)
    return np.moveaxis((codes * scale).reshape(v.shape), -1, axis)


WIDE = False


def mx_kscale(k):
    if not WIDE:
        return np.ones(k)
    levels = np.array([10, -10, 5, -5, 0])
    if k % 512:
        return np.exp2(np.random.permutation(np.resize(levels, k // 32))).repeat(32)
    a = np.empty((k // 512, 16))
    for p in range(k // 512):
        a[p, :8] = np.random.permutation(np.resize(levels, 8))
        for g in range(8):
            far = levels[np.abs(levels - a[p, g]) >= 10]
            a[p, g + 8] = far[np.random.randint(len(far))]
    return np.exp2(a.ravel()).repeat(32)


def f64(x):
    return np.asarray(x).astype(np.float64)


def striped(idx):
    return np.tile(idx.reshape(-1, 16).T, (8, 1)).astype(np.uint16)


def unstriped(offs):
    return offs[:16].T.reshape(-1).astype(np.int64)


def pack_weight(w):
    k, n = w.shape
    w = f64(np.asarray(w, np.float32).astype(ml_dtypes.bfloat16)).reshape(k // 32, 32, n)
    amax = np.abs(w).max(1)
    byte = np.clip(np.where(amax > 0, np.frexp(amax)[1] - 1 + 127 - 7, 1), 1, 254)
    scaled = (w * np.exp2(127.0 - byte)[:, None, :]).reshape(k, n).astype(np.float32)
    words = np.ascontiguousarray(scaled.reshape(k // 512, 128, 4, n).transpose(0, 1, 3, 2)).astype(ml_dtypes.float8_e4m3fn).view(np.uint8)
    return words, np.ascontiguousarray(byte.astype(np.uint8).reshape(k // 512, 16, n))


def unpack_weight(words, scales):
    g, p, n, _ = words.shape
    vals = np.ascontiguousarray(words).view(ml_dtypes.float8_e4m3fn).astype(np.float64) * np.repeat(np.exp2(scales.astype(np.float64) - 127.0), 8, axis=1)[..., None]
    return vals.transpose(0, 1, 3, 2).reshape(g * 512, n)


K, T, D, S, V, N = 1024, 1024, 2, 512, 256, 256


def setup_inputs():
    n = np.random.standard_normal
    s = mx_kscale(K)[:, None]
    words, scales = pack_weight(n((K, N)) / np.sqrt(K) / s)
    return {
        "xT": (n((K, T)) * s).astype(np.float32),
        "w_words": words,
        "w_scales": scales,
        "b": (0.3 * n((N, 1))).astype(np.float32),
        "gate": np.tile(np.random.uniform(0.2, 1.0, (D, 1, V)) / np.sqrt(D), (1, N, 1)).astype(np.float32),
        "offs": striped(np.random.permutation(T)[:S]),
        "pos1": striped(np.random.permutation(S)[:V]),
        "pos2": striped(np.random.permutation(S)[:V]),
    }


def reference(xT, w_words, w_scales, b, gate, offs, pos1, pos2):
    w = unpack_weight(w_words, w_scales)
    idx = unstriped(offs)
    xq = mxq(f64(xT)[:, idx], 0, "e4m3")
    y = w.T @ xq
    y = y + f64(b)
    return sum(f64(gate[d]) * y[:, unstriped(p)] for d, p in enumerate((pos1, pos2)))

@@ -1,0 +1,156 @@
+from contextlib import ExitStack
+
+import concourse.mybir as mybir
+
+F32 = mybir.dt.float32
+BF16 = mybir.dt.bfloat16
+U32 = mybir.dt.uint32
+I32 = mybir.dt.int32
+U16 = mybir.dt.uint16
+U8 = mybir.dt.uint8
+FP8X4 = mybir.dt.float8_e4m3fn_x4
+MULT = mybir.AluOpType.mult
+ADD = mybir.AluOpType.add
+IDENTITY = mybir.ActivationFunctionType.Identity
+
+P = 128
+K, T, S, V, N, D = 1024, 1024, 512, 256, 256, 2
+PASSES = K // 512
+BLOCKS = N // P
+HALF = S // 2
+
+FLOPS = 2 * K * S * N + 3 * N * V
+
+
+def tile_picked_sub_lin_bias_sub_e_kernel(tc, xT, w_words, w_scales, b, gate, offs, pos1, pos2, out):
+    nc = tc.nc
+    with ExitStack() as ctx:
+        held = ctx.enter_context(tc.tile_pool(name="held", bufs=1))
+        psum = ctx.enter_context(tc.psum_pool(name="psum", bufs=1))
+
+        offs_sb = held.tile([P, S // 16], U16, name="offs_sb")
+        pos_sb = [held.tile([P, V // 16], U16, name=f"pos_sb{d}") for d in range(D)]
+
+        raw = [[held.tile([P, 2, T], F32, name=f"raw{a}{u}") for u in range(2)] for a in range(PASSES)]
+        pairs = [[held.tile([P, T, 2], BF16, name=f"pairs{a}{u}", align_bytes=64) for u in range(2)] for a in range(PASSES)]
+        grouped = [held.tile([P, 4 * S], BF16, name=f"grouped{a}", align_bytes=64) for a in range(PASSES)]
+        codes = [held.tile([P, S], U32, name=f"codes{a}", align_bytes=64) for a in range(PASSES)]
+        scales = [held.tile([P, S], U8, name=f"scales{a}", align_bytes=64) for a in range(PASSES)]
+        w_codes = held.tile([P, PASSES, N], U32, name="w_codes", align_bytes=64)
+        w_sc = held.tile([P, N], U8, name="w_sc", align_bytes=64)
+        bias = held.tile([P, BLOCKS], F32, name="bias")
+        gates = held.tile([P, BLOCKS, D, V], F32, name="gates")
+        y = [held.tile([P, S], F32, name=f"y{c}") for c in range(BLOCKS)]
+
+        nc.gpsimd.memset(w_sc[:].bitcast(I32), 0)
+        for q in range(4):
+            nc.gpsimd.dma_start(
+                out=w_sc[32 * q : 32 * q + 8, :].bitcast(I32), in_=w_scales[:, 4 * q : 4 * q + 4, :].bitcast(I32)
+            )
+        nc.gpsimd.dma_start(out=bias[:], in_=b.rearrange("(c p) o -> p (c o)", c=BLOCKS))
+
+        x_rows = xT.rearrange("(a p u e) t -> a u p e t", a=PASSES, u=2, e=2)
+        chunks = []
+        for a in range(PASSES):
+            for u in range(2):
+                widths = (512, 256, 256) if a == PASSES - 1 and u == 1 else (512, 512)
+                t0 = 0
+                for width in widths:
+                    chunks.append((a, u, t0, t0 + width))
+                    t0 += width
+        for i, (a, u, t0, t1) in enumerate(chunks):
+            nc.sync.dma_start(out=raw[a][u][:, :, t0:t1], in_=x_rows[a, u][:, :, t0:t1])
+            if i == 0:
+                nc.sync.dma_start(offs_sb[:], offs)
+        nc.sync.dma_start(
+            out=w_codes[:].rearrange("p a n -> p (a n)").bitcast(I32).rearrange("p (a n) -> p a n", a=PASSES),
+            in_=w_words.rearrange("a p n r -> p a (n r)").bitcast(I32),
+        )
+        nc.sync.dma_start(pos_sb[0][:], pos1)
+        nc.sync.dma_start(pos_sb[1][:], pos2)
+        for c in range(BLOCKS):
+            nc.sync.dma_start(out=gates[:, c, :, :], in_=gate[:, c * P : (c + 1) * P, :].rearrange("d p v -> p d v"))
+
+        acc = [[psum.tile([P, HALF], F32, name=f"acc{c}{h}") for h in range(2)] for c in range(BLOCKS)]
+
+        def cast(engine, i):
+            a, u, t0, t1 = chunks[i]
+            dst = pairs[a][u][:, t0:t1, :]
+            src = raw[a][u][:, :, t0:t1].rearrange("p e t -> p t e")
+            if engine == "v":
+                nc.vector.tensor_copy(out=dst, in_=src)
+            else:
+                nc.scalar.copy(out=dst, in_=src)
+
+        def gather(a, u, h0, h1):
+            window = pairs[a][u][:].rearrange("p t e -> p (t e)").bitcast(U32)
+            dst = grouped[a][:].bitcast(U32).rearrange("p (n u) -> p n u", u=2)[:, h0:h1, u]
+            nc.vector.tensor_copy(out=dst, in_=window.indirect(offs_sb[:, h0 // 16 : h1 // 16]))
+
+        def quantise(a, h0, h1):
+            nc.vector.quantize_mx(
+                out=codes[a][:, h0:h1].bitcast(FP8X4), scales=scales[a][:, h0:h1], in_=grouped[a][:, 4 * h0 : 4 * h1]
+            )
+
+        def multiply(a, c, h):
+            nc.tensor.matmul_mx(
+                out=acc[c][h][:],
+                lhsT=w_codes[:, a, c * P : (c + 1) * P].bitcast(FP8X4),
+                lhsT_scale=w_sc[4 * a :, c * P : (c + 1) * P],
+                rhs=codes[a][:, h * HALF : (h + 1) * HALF].bitcast(FP8X4),
+                rhs_scale=scales[a][:, h * HALF : (h + 1) * HALF],
+                start=(a == 0),
+                stop=(a == PASSES - 1),
+            )
+
+        def add_bias(engine, c, h):
+            dst = y[c][:, h * HALF : (h + 1) * HALF]
+            if engine == "v":
+                nc.vector.tensor_scalar(dst, acc[c][h][:], bias[:, c : c + 1], None, ADD)
+            else:
+                nc.scalar.activation(dst, acc[c][h][:], IDENTITY, bias=bias[:, c : c + 1])
+
+        cast("v", 0)
+        cast("v", 1)
+        gather(0, 0, 0, S)
+        cast("s", 2)
+        cast("v", 3)
+        gather(0, 1, 0, S)
+        cast("s", 4)
+        cast("s", 5)
+        quantise(0, 0, S)
+        gather(1, 0, 0, S)
+        for c in range(BLOCKS):
+            for h in range(2):
+                multiply(0, c, h)
+        cast("s", 6)
+        cast("s", 7)
+        cast("v", 8)
+        gather(1, 1, 0, HALF)
+        gather(1, 1, HALF, S)
+        quantise(1, 0, HALF)
+        quantise(1, HALF, S)
+        multiply(1, 0, 0)
+        multiply(1, 1, 0)
+        multiply(1, 0, 1)
+        multiply(1, 1, 1)
+        add_bias("s", 0, 0)
+        add_bias("v", 1, 0)
+        add_bias("s", 0, 1)
+        add_bias("s", 1, 1)
+
+        def look_up(c, d):
+            term = held.tile([P, V], F32, name=f"term{c}{d}")
+            nc.vector.tensor_tensor(term[:], y[c][:].indirect(pos_sb[d][:]), gates[:, c, d, :], MULT)
+            return term
+
+        def finish(c, terms):
+            result = held.tile([P, V], F32, name=f"result{c}")
+            nc.vector.tensor_tensor(result[:], terms[0][:], terms[1][:], ADD)
+            nc.sync.dma_start(out=out[c * P : (c + 1) * P, :], in_=result[:])
+
+        first = [look_up(0, 0), look_up(0, 1)]
+        second = [look_up(1, 0)]
+        finish(0, first)
+        second.append(look_up(1, 1))
+        finish(1, second)

@@ -18,6 +18,7 @@ K, T, S, V, N, D = 1024, 1024, 512, 256, 256, 2
 PASSES = K // 512
 BLOCKS = N // P
 HALF = S // 2
+CUTS = (((0, 256), (256, 384), (384, S)), ((0, 256), (256, S)))
 
 FLOPS = 2 * K * S * N + 3 * N * V
 
@@ -42,39 +43,27 @@ def tile_picked_sub_lin_bias_sub_e_kernel(tc, xT, w_words, w_scales, b, gate, of
         gates = held.tile([P, BLOCKS, D, V], F32, name="gates")
         y = [held.tile([P, S], F32, name=f"y{c}") for c in range(BLOCKS)]
 
-        nc.gpsimd.memset(w_sc[:].bitcast(I32), 0)
-        for q in range(4):
-            nc.gpsimd.dma_start(
-                out=w_sc[32 * q : 32 * q + 8, :].bitcast(I32), in_=w_scales[:, 4 * q : 4 * q + 4, :].bitcast(I32)
-            )
-        nc.gpsimd.dma_start(out=bias[:], in_=b.rearrange("(c p) o -> p (c o)", c=BLOCKS))
-
+        nc.vector.memset(w_sc[:].bitcast(I32), 0)
         x_rows = xT.rearrange("(a p u e) t -> a u p e t", a=PASSES, u=2, e=2)
-        chunks = []
-        for a in range(PASSES):
-            for u in range(2):
-                widths = (512, 256, 256) if a == PASSES - 1 and u == 1 else (512, 512)
-                t0 = 0
-                for width in widths:
-                    chunks.append((a, u, t0, t0 + width))
-                    t0 += width
-        for i, (a, u, t0, t1) in enumerate(chunks):
+        nc.sync.dma_start(offs_sb[:], offs)
+        for a, u, t0, t1 in ((0, 0, 0, T), (0, 1, 0, T), (1, 0, 0, 512), (1, 0, 512, T), (1, 1, 0, 512), (1, 1, 512, 768), (1, 1, 768, T)):
             nc.sync.dma_start(out=raw[a][u][:, :, t0:t1], in_=x_rows[a, u][:, :, t0:t1])
-            if i == 0:
-                nc.sync.dma_start(offs_sb[:], offs)
-        nc.sync.dma_start(
-            out=w_codes[:].rearrange("p a n -> p (a n)").bitcast(I32).rearrange("p (a n) -> p a n", a=PASSES),
-            in_=w_words.rearrange("a p n r -> p a (n r)").bitcast(I32),
-        )
+            if a == 0 and u == 0 and t1 == T:
+                for q in range(4):
+                    nc.sync.dma_start(
+                        out=w_sc[32 * q : 32 * q + 8, :].bitcast(I32),
+                        in_=w_scales[:, 4 * q : 4 * q + 4, :].bitcast(I32),
+                    )
+                nc.sync.dma_start(out=bias[:], in_=b.rearrange("(c p) o -> p (c o)", c=BLOCKS))
+        nc.sync.dma_start(out=w_codes[:].bitcast(I32), in_=w_words.rearrange("a p n r -> p a (n r)").bitcast(I32))
         nc.sync.dma_start(pos_sb[0][:], pos1)
         nc.sync.dma_start(pos_sb[1][:], pos2)
         for c in range(BLOCKS):
             nc.sync.dma_start(out=gates[:, c, :, :], in_=gate[:, c * P : (c + 1) * P, :].rearrange("d p v -> p d v"))
 
-        acc = [[psum.tile([P, HALF], F32, name=f"acc{c}{h}") for h in range(2)] for c in range(BLOCKS)]
+        acc = [[psum.tile([P, n1 - n0], F32, name=f"acc{c}{i}") for i, (n0, n1) in enumerate(CUTS[c])] for c in range(BLOCKS)]
 
-        def cast(engine, i):
-            a, u, t0, t1 = chunks[i]
+        def cast(engine, a, u, t0, t1):
             dst = pairs[a][u][:, t0:t1, :]
             src = raw[a][u][:, :, t0:t1].rearrange("p e t -> p t e")
             if engine == "v":
@@ -83,60 +72,65 @@ def tile_picked_sub_lin_bias_sub_e_kernel(tc, xT, w_words, w_scales, b, gate, of
                 nc.scalar.copy(out=dst, in_=src)
 
         def gather(a, u, h0, h1):
+            offsets = offs_sb[:] if h1 - h0 == S else offs_sb[:, h0 // 16 : h1 // 16]
             window = pairs[a][u][:].rearrange("p t e -> p (t e)").bitcast(U32)
             dst = grouped[a][:].bitcast(U32).rearrange("p (n u) -> p n u", u=2)[:, h0:h1, u]
-            nc.vector.tensor_copy(out=dst, in_=window.indirect(offs_sb[:, h0 // 16 : h1 // 16]))
+            nc.vector.tensor_copy(out=dst, in_=window.indirect(offsets))
 
         def quantise(a, h0, h1):
             nc.vector.quantize_mx(
                 out=codes[a][:, h0:h1].bitcast(FP8X4), scales=scales[a][:, h0:h1], in_=grouped[a][:, 4 * h0 : 4 * h1]
             )
 
-        def multiply(a, c, h):
+        def multiply(a, c, i):
+            n0, n1 = CUTS[c][i]
             nc.tensor.matmul_mx(
-                out=acc[c][h][:],
+                out=acc[c][i][:],
                 lhsT=w_codes[:, a, c * P : (c + 1) * P].bitcast(FP8X4),
                 lhsT_scale=w_sc[4 * a :, c * P : (c + 1) * P],
-                rhs=codes[a][:, h * HALF : (h + 1) * HALF].bitcast(FP8X4),
-                rhs_scale=scales[a][:, h * HALF : (h + 1) * HALF],
+                rhs=codes[a][:, n0:n1].bitcast(FP8X4),
+                rhs_scale=scales[a][:, n0:n1],
                 start=(a == 0),
                 stop=(a == PASSES - 1),
             )
 
-        def add_bias(engine, c, h):
-            dst = y[c][:, h * HALF : (h + 1) * HALF]
+        def add_bias(engine, c, i):
+            n0, n1 = CUTS[c][i]
+            dst = y[c][:, n0:n1]
             if engine == "v":
-                nc.vector.tensor_scalar(dst, acc[c][h][:], bias[:, c : c + 1], None, ADD)
+                nc.vector.tensor_scalar(dst, acc[c][i][:], bias[:, c : c + 1], None, ADD)
             else:
-                nc.scalar.activation(dst, acc[c][h][:], IDENTITY, bias=bias[:, c : c + 1])
+                nc.scalar.activation(dst, acc[c][i][:], IDENTITY, bias=bias[:, c : c + 1])
 
-        cast("v", 0)
-        cast("v", 1)
+        cast("s", 0, 0, 0, 416)
+        cast("v", 0, 0, 416, T)
         gather(0, 0, 0, S)
-        cast("s", 2)
-        cast("v", 3)
+        cast("s", 0, 1, 0, 512)
+        cast("v", 0, 1, 512, T)
         gather(0, 1, 0, S)
-        cast("s", 4)
-        cast("s", 5)
+        cast("s", 1, 0, 0, 512)
+        cast("s", 1, 0, 512, T)
         quantise(0, 0, S)
         gather(1, 0, 0, S)
         for c in range(BLOCKS):
-            for h in range(2):
-                multiply(0, c, h)
-        cast("s", 6)
-        cast("s", 7)
-        cast("v", 8)
+            for i in range(len(CUTS[c])):
+                multiply(0, c, i)
+        cast("s", 1, 1, 0, 512)
+        cast("s", 1, 1, 512, 768)
+        cast("v", 1, 1, 768, T)
         gather(1, 1, 0, HALF)
         gather(1, 1, HALF, S)
-        quantise(1, 0, HALF)
-        quantise(1, HALF, S)
+        for n0, n1 in CUTS[0]:
+            quantise(1, n0, n1)
         multiply(1, 0, 0)
-        multiply(1, 1, 0)
         multiply(1, 0, 1)
+        multiply(1, 0, 2)
+        multiply(1, 1, 0)
         multiply(1, 1, 1)
         add_bias("s", 0, 0)
-        add_bias("v", 1, 0)
         add_bias("s", 0, 1)
+        add_bias("v", 0, 2)
+        add_bias("s", 1, 0)
         add_bias("s", 1, 1)
 
         def look_up(c, d):
@@ -150,7 +144,6 @@ def tile_picked_sub_lin_bias_sub_e_kernel(tc, xT, w_words, w_scales, b, gate, of
             nc.sync.dma_start(out=out[c * P : (c + 1) * P, :], in_=result[:])
 
         first = [look_up(0, 0), look_up(0, 1)]
-        second = [look_up(1, 0)]
+        second = [look_up(1, 0), look_up(1, 1)]
         finish(0, first)
-        second.append(look_up(1, 1))
         finish(1, second)

@@ -45,21 +45,24 @@ def tile_picked_sub_lin_bias_sub_e_kernel(tc, xT, w_words, w_scales, b, gate, of
 
         nc.vector.memset(w_sc[:].bitcast(I32), 0)
         x_rows = xT.rearrange("(a p u e) t -> a u p e t", a=PASSES, u=2, e=2)
-        nc.sync.dma_start(offs_sb[:], offs)
-        for a, u, t0, t1 in ((0, 0, 0, T), (0, 1, 0, T), (1, 0, 0, 512), (1, 0, 512, T), (1, 1, 0, 512), (1, 1, 512, 768), (1, 1, 768, T)):
+        loads = ((0, 0, 0, T), (0, 1, 0, T), (1, 0, 0, 512), (1, 0, 512, T), (1, 1, 0, 512), (1, 1, 512, 768), (1, 1, 768, T))
+        for i, (a, u, t0, t1) in enumerate(loads):
             nc.sync.dma_start(out=raw[a][u][:, :, t0:t1], in_=x_rows[a, u][:, :, t0:t1])
-            if a == 0 and u == 0 and t1 == T:
-                for q in range(4):
-                    nc.sync.dma_start(
-                        out=w_sc[32 * q : 32 * q + 8, :].bitcast(I32),
-                        in_=w_scales[:, 4 * q : 4 * q + 4, :].bitcast(I32),
-                    )
-                nc.sync.dma_start(out=bias[:], in_=b.rearrange("(c p) o -> p (c o)", c=BLOCKS))
+            if i == 0:
+                nc.sync.dma_start(offs_sb[:], offs)
+            if i == 3:
+                nc.sync.dma_start(pos_sb[0][:], pos1)
+                nc.sync.dma_start(pos_sb[1][:], pos2)
         nc.sync.dma_start(out=w_codes[:].bitcast(I32), in_=w_words.rearrange("a p n r -> p a (n r)").bitcast(I32))
-        nc.sync.dma_start(pos_sb[0][:], pos1)
-        nc.sync.dma_start(pos_sb[1][:], pos2)
-        for c in range(BLOCKS):
-            nc.sync.dma_start(out=gates[:, c, :, :], in_=gate[:, c * P : (c + 1) * P, :].rearrange("d p v -> p d v"))
+        for q in range(4):
+            nc.sync.dma_start(
+                out=w_sc[32 * q : 32 * q + 8, :].bitcast(I32),
+                in_=w_scales[:, 4 * q : 4 * q + 4, :].bitcast(I32),
+            )
+        gate_rows = gate.rearrange("d (c p) v -> c p d v", c=BLOCKS)
+        nc.sync.dma_start(out=gates[:, 0, :, :], in_=gate_rows[0])
+        nc.sync.dma_start(out=bias[:], in_=b.rearrange("(c p) o -> p (c o)", c=BLOCKS))
+        nc.sync.dma_start(out=gates[:, 1, :, :], in_=gate_rows[1])
 
         acc = [[psum.tile([P, n1 - n0], F32, name=f"acc{c}{i}") for i, (n0, n1) in enumerate(CUTS[c])] for c in range(BLOCKS)]
 
@@ -105,8 +108,8 @@ def tile_picked_sub_lin_bias_sub_e_kernel(tc, xT, w_words, w_scales, b, gate, of
         cast("s", 0, 0, 0, 416)
         cast("v", 0, 0, 416, T)
         gather(0, 0, 0, S)
-        cast("s", 0, 1, 0, 512)
-        cast("v", 0, 1, 512, T)
+        cast("s", 0, 1, 0, 480)
+        cast("v", 0, 1, 480, T)
         gather(0, 1, 0, S)
         cast("s", 1, 0, 0, 512)
         cast("s", 1, 0, 512, T)

from contextlib import ExitStack

import concourse.mybir as mybir

F32 = mybir.dt.float32
BF16 = mybir.dt.bfloat16
U32 = mybir.dt.uint32
I32 = mybir.dt.int32
U16 = mybir.dt.uint16
U8 = mybir.dt.uint8
FP8X4 = mybir.dt.float8_e4m3fn_x4
MULT = mybir.AluOpType.mult
ADD = mybir.AluOpType.add
IDENTITY = mybir.ActivationFunctionType.Identity

P = 128
K, T, S, V, N, D = 1024, 1024, 512, 256, 256, 2
PASSES = K // 512
BLOCKS = N // P
HALF = S // 2
CUTS = (((0, 256), (256, 384), (384, S)), ((0, 256), (256, S)))

FLOPS = 2 * K * S * N + 3 * N * V


def tile_picked_sub_lin_bias_sub_e_kernel(tc, xT, w_words, w_scales, b, gate, offs, pos1, pos2, out):
    nc = tc.nc
    with ExitStack() as ctx:
        held = ctx.enter_context(tc.tile_pool(name="held", bufs=1))
        psum = ctx.enter_context(tc.psum_pool(name="psum", bufs=1))

        offs_sb = held.tile([P, S // 16], U16, name="offs_sb")
        pos_sb = [held.tile([P, V // 16], U16, name=f"pos_sb{d}") for d in range(D)]

        raw = [[held.tile([P, 2, T], F32, name=f"raw{a}{u}") for u in range(2)] for a in range(PASSES)]
        pairs = [[held.tile([P, T, 2], BF16, name=f"pairs{a}{u}", align_bytes=64) for u in range(2)] for a in range(PASSES)]
        grouped = [held.tile([P, 4 * S], BF16, name=f"grouped{a}", align_bytes=64) for a in range(PASSES)]
        codes = [held.tile([P, S], U32, name=f"codes{a}", align_bytes=64) for a in range(PASSES)]
        scales = [held.tile([P, S], U8, name=f"scales{a}", align_bytes=64) for a in range(PASSES)]
        w_codes = held.tile([P, PASSES, N], U32, name="w_codes", align_bytes=64)
        w_sc = held.tile([P, N], U8, name="w_sc", align_bytes=64)
        bias = held.tile([P, BLOCKS], F32, name="bias")
        gates = held.tile([P, BLOCKS, D, V], F32, name="gates")
        y = [held.tile([P, S], F32, name=f"y{c}") for c in range(BLOCKS)]

        nc.vector.memset(w_sc[:].bitcast(I32), 0)
        x_rows = xT.rearrange("(a p u e) t -> a u p e t", a=PASSES, u=2, e=2)
        loads = ((0, 0, 0, T), (0, 1, 0, T), (1, 0, 0, 512), (1, 0, 512, T), (1, 1, 0, 512), (1, 1, 512, 768), (1, 1, 768, T))
        for i, (a, u, t0, t1) in enumerate(loads):
            nc.sync.dma_start(out=raw[a][u][:, :, t0:t1], in_=x_rows[a, u][:, :, t0:t1])
            if i == 0:
                nc.sync.dma_start(offs_sb[:], offs)
            if i == 3:
                nc.sync.dma_start(pos_sb[0][:], pos1)
                nc.sync.dma_start(pos_sb[1][:], pos2)
        nc.sync.dma_start(out=w_codes[:].bitcast(I32), in_=w_words.rearrange("a p n r -> p a (n r)").bitcast(I32))
        for q in range(4):
            nc.sync.dma_start(
                out=w_sc[32 * q : 32 * q + 8, :].bitcast(I32),
                in_=w_scales[:, 4 * q : 4 * q + 4, :].bitcast(I32),
            )
        gate_rows = gate.rearrange("d (c p) v -> c p d v", c=BLOCKS)
        nc.sync.dma_start(out=gates[:, 0, :, :], in_=gate_rows[0])
        nc.sync.dma_start(out=bias[:], in_=b.rearrange("(c p) o -> p (c o)", c=BLOCKS))
        nc.sync.dma_start(out=gates[:, 1, :, :], in_=gate_rows[1])

        acc = [[psum.tile([P, n1 - n0], F32, name=f"acc{c}{i}") for i, (n0, n1) in enumerate(CUTS[c])] for c in range(BLOCKS)]

        def cast(engine, a, u, t0, t1):
            dst = pairs[a][u][:, t0:t1, :]
            src = raw[a][u][:, :, t0:t1].rearrange("p e t -> p t e")
            if engine == "v":
                nc.vector.tensor_copy(out=dst, in_=src)
            else:
                nc.scalar.copy(out=dst, in_=src)

        def gather(a, u, h0, h1):
            offsets = offs_sb[:] if h1 - h0 == S else offs_sb[:, h0 // 16 : h1 // 16]
            window = pairs[a][u][:].rearrange("p t e -> p (t e)").bitcast(U32)
            dst = grouped[a][:].bitcast(U32).rearrange("p (n u) -> p n u", u=2)[:, h0:h1, u]
            nc.vector.tensor_copy(out=dst, in_=window.indirect(offsets))

        def quantise(a, h0, h1):
            nc.vector.quantize_mx(
                out=codes[a][:, h0:h1].bitcast(FP8X4), scales=scales[a][:, h0:h1], in_=grouped[a][:, 4 * h0 : 4 * h1]
            )

        def multiply(a, c, i):
            n0, n1 = CUTS[c][i]
            nc.tensor.matmul_mx(
                out=acc[c][i][:],
                lhsT=w_codes[:, a, c * P : (c + 1) * P].bitcast(FP8X4),
                lhsT_scale=w_sc[4 * a :, c * P : (c + 1) * P],
                rhs=codes[a][:, n0:n1].bitcast(FP8X4),
                rhs_scale=scales[a][:, n0:n1],
                start=(a == 0),
                stop=(a == PASSES - 1),
            )

        def add_bias(engine, c, i):
            n0, n1 = CUTS[c][i]
            dst = y[c][:, n0:n1]
            if engine == "v":
                nc.vector.tensor_scalar(dst, acc[c][i][:], bias[:, c : c + 1], None, ADD)
            else:
                nc.scalar.activation(dst, acc[c][i][:], IDENTITY, bias=bias[:, c : c + 1])

        cast("s", 0, 0, 0, 416)
        cast("v", 0, 0, 416, T)
        gather(0, 0, 0, S)
        cast("s", 0, 1, 0, 480)
        cast("v", 0, 1, 480, T)
        gather(0, 1, 0, S)
        cast("s", 1, 0, 0, 512)
        cast("s", 1, 0, 512, T)
        quantise(0, 0, S)
        gather(1, 0, 0, S)
        for c in range(BLOCKS):
            for i in range(len(CUTS[c])):
                multiply(0, c, i)
        cast("s", 1, 1, 0, 512)
        cast("s", 1, 1, 512, 768)
        cast("v", 1, 1, 768, T)
        gather(1, 1, 0, HALF)
        gather(1, 1, HALF, S)
        for n0, n1 in CUTS[0]:
            quantise(1, n0, n1)
        multiply(1, 0, 0)
        multiply(1, 0, 1)
        multiply(1, 0, 2)
        multiply(1, 1, 0)
        multiply(1, 1, 1)
        add_bias("s", 0, 0)
        add_bias("s", 0, 1)
        add_bias("v", 0, 2)
        add_bias("s", 1, 0)
        add_bias("s", 1, 1)

        def look_up(c, d):
            term = held.tile([P, V], F32, name=f"term{c}{d}")
            nc.vector.tensor_tensor(term[:], y[c][:].indirect(pos_sb[d][:]), gates[:, c, d, :], MULT)
            return term

        def finish(c, terms):
            result = held.tile([P, V], F32, name=f"result{c}")
            nc.vector.tensor_tensor(result[:], terms[0][:], terms[1][:], ADD)
            nc.sync.dma_start(out=out[c * P : (c + 1) * P, :], in_=result[:])

        first = [look_up(0, 0), look_up(0, 1)]
        second = [look_up(1, 0), look_up(1, 1)]
        finish(0, first)
        finish(1, second)
